import numpy as np
import ml_dtypes


def mxq(x, axis, fmt="e4m3"):
    dtype, down = {"e4m3": (ml_dtypes.float8_e4m3fn, 7), "e5m2": (ml_dtypes.float8_e5m2, 14)}[fmt]
    v = np.moveaxis(np.asarray(x, np.float32).astype(ml_dtypes.bfloat16).astype(np.float64), axis, -1)
    blocks = v.reshape(v.shape[:-1] + (-1, 32))
    amax = np.abs(blocks).max(-1, keepdims=True)
    byte = np.maximum(np.where(amax > 0, np.frexp(amax)[1] - 1 + 127, 0) - down, 1)
    scale = np.exp2(byte - 127.0)
    codes = (blocks / scale).astype(np.float32).astype(dtype).astype(np.float64)
    return np.moveaxis((codes * scale).reshape(v.shape), -1, axis)


WIDE = False


def mx_kscale(k):
    if not WIDE:
        return np.ones(k)
    levels = np.array([10, -10, 5, -5, 0])
    if k % 512:
        return np.exp2(np.random.permutation(np.resize(levels, k // 32))).repeat(32)
    a = np.empty((k // 512, 16))
    for p in range(k // 512):
        a[p, :8] = np.random.permutation(np.resize(levels, 8))
        for g in range(8):
            far = levels[np.abs(levels - a[p, g]) >= 10]
            a[p, g + 8] = far[np.random.randint(len(far))]
    return np.exp2(a.ravel()).repeat(32)


def f64(x):
    return np.asarray(x).astype(np.float64)


def striped(idx):
    return np.tile(idx.reshape(-1, 16).T, (8, 1)).astype(np.uint16)


def unstriped(offs):
    return offs[:16].T.reshape(-1).astype(np.int64)


def pack_weight(w):
    k, n = w.shape
    w = f64(np.asarray(w, np.float32).astype(ml_dtypes.bfloat16)).reshape(k // 32, 32, n)
    amax = np.abs(w).max(1)
    byte = np.clip(np.where(amax > 0, np.frexp(amax)[1] - 1 + 127 - 7, 1), 1, 254)
    scaled = (w * np.exp2(127.0 - byte)[:, None, :]).reshape(k, n).astype(np.float32)
    words = np.ascontiguousarray(scaled.reshape(k // 512, 128, 4, n).transpose(0, 1, 3, 2)).astype(ml_dtypes.float8_e4m3fn).view(np.uint8)
    return words, np.ascontiguousarray(byte.astype(np.uint8).reshape(k // 512, 16, n))


def unpack_weight(words, scales):
    g, p, n, _ = words.shape
    vals = np.ascontiguousarray(words).view(ml_dtypes.float8_e4m3fn).astype(np.float64) * np.repeat(np.exp2(scales.astype(np.float64) - 127.0), 8, axis=1)[..., None]
    return vals.transpose(0, 1, 3, 2).reshape(g * 512, n)


def planes(y):
    n, m = y.shape
    v = y.astype(np.float32).astype(ml_dtypes.bfloat16).astype(np.float64).reshape(n // 32, 32, m)
    top = np.abs(v).max(1)
    byte = np.clip(np.where(top > 0, np.frexp(top)[1] - 1 + 127 - 7, 1), 1, 254)
    codes = (v * np.exp2(127.0 - byte)[:, None, :]).reshape(n, m).astype(np.float32).astype(ml_dtypes.float8_e4m3fn).view(np.uint8)
    words = codes.reshape(n // 512, 128, 4, m).transpose(0, 1, 3, 2)
    return np.ascontiguousarray(words), np.ascontiguousarray(byte.astype(np.uint8).reshape(n // 512, 16, m))


def relu(v):
    return np.maximum(v, 0.0)


K, T, S, V, H, N, D, W = 512, 1024, 512, 256, 512, 512, 3, 1024
P = 2 ** 7


def setup_inputs():
    n = np.random.standard_normal
    s = mx_kscale(K)[:, None]
    u = mx_kscale(H)
    near = np.random.permutation(S)
    packed_xT = pack_weight(n((K, T)) * s)
    packed_eT = pack_weight(n((K, W)) * s)
    return {
        "x_words": packed_xT[0],
        "x_scales": packed_xT[1],
        "e_words": packed_eT[0],
        "e_scales": packed_eT[1],
        "w1": (n((K, H)) / np.sqrt(K) / s * u).astype(np.float32),
        "w2": (n((K, H)) / np.sqrt(K) / s).astype(np.float32),
        "w3": (n((H, N)) / np.sqrt(2 * H) / u[:, None]).astype(np.float32),
        "w4": (n((H, N)) / np.sqrt(2 * H) / u[:, None]).astype(np.float32),
        "gate": (np.tile(np.random.uniform(0.3, 0.9, (D, 1, V)), (1, P, 1))).astype(np.float32),
        "offs": striped(np.random.permutation(T)[:S]),
        "usr": striped(np.random.permutation(W)[:V]),
        "pos1": striped(near[:V]),
        "pos2": striped(near[V:]),
        "pos3": striped(np.random.permutation(S)[:V]),
    }


def reference(x_words, x_scales, e_words, e_scales, w1, w2, w3, w4, gate, offs, usr, pos1, pos2, pos3):
    xq = unpack_weight(x_words, x_scales)[:, unstriped(offs)]
    h = mxq(f64(w1), 0, "e4m3").T @ xq
    z = h[:, unstriped(pos1)] * f64(gate)[0, :1] + h[:, unstriped(pos2)] * f64(gate)[1, :1] + h[:, unstriped(pos3)] * f64(gate)[2, :1]
    e_usr = unpack_weight(e_words, e_scales)[:, unstriped(usr)]
    gg = mxq(f64(w2), 0, "e4m3").T @ e_usr
    y = z * gg
    out_0 = relu(mxq(f64(w3), 0, "e4m3").T @ mxq(z, 0, "e4m3") + mxq(f64(w4), 0, "e4m3").T @ mxq(y, 0, "e4m3"))
    return (out_0,) + planes(out_0)

@@ -1,0 +1,218 @@
+from contextlib import ExitStack
+
+import concourse.mybir as mybir
+
+K, T, S, V, H, N, D = 512, 1024, 512, 256, 512, 512, 3
+FLOPS = 2 * K * H * S + 2 * K * H * V + 2 * 2 * H * N * V
+
+F32 = mybir.dt.float32
+BF16 = mybir.dt.bfloat16
+I32 = mybir.dt.int32
+U32 = mybir.dt.uint32
+U16 = mybir.dt.uint16
+U8 = mybir.dt.uint8
+FP8X4 = mybir.dt.float8_e4m3fn_x4
+MULT = mybir.AluOpType.mult
+ADD = mybir.AluOpType.add
+COPY = mybir.ActivationFunctionType.Copy
+RELU = mybir.ActivationFunctionType.Relu
+
+P = 128
+PACK = 4
+VH = 128
+HALVES = V // VH
+LIST_COLS = VH // 16
+
+
+def tile_picked_yngcf_relu_po_kernel(
+    tc, x_words, x_scales, e_words, e_scales, w1, w2, w3, w4, gate, offs, usr, pos1, pos2, pos3, out_0, out_1, out_2
+):
+    nc = tc.nc
+    with ExitStack() as ctx:
+        sb = ctx.enter_context(tc.tile_pool(name="sb", bufs=1))
+        ps = ctx.enter_context(tc.psum_pool(name="ps", bufs=1))
+
+        def load_list(src, name):
+            tile = sb.tile(list(src.shape), U16, name=name)
+            nc.sync.dma_start(tile[:], src)
+            return tile
+
+        def load_words(src, name):
+            tile = sb.tile([P, T], U32, name=name, align_bytes=64)
+            nc.sync.dma_start(tile[:].bitcast(I32), src[0].rearrange("p c r -> p (c r)").bitcast(I32))
+            return tile
+
+        def load_scales(src, name, queue):
+            tile = sb.tile([P, T], U8, name=name, align_bytes=64)
+            nc.vector.memset(tile[:].bitcast(I32), 0)
+            for q in range(4):
+                queue.dma_start(tile[32 * q : 32 * q + 4, :].bitcast(I32), src[0, 4 * q : 4 * q + 4, :].bitcast(I32))
+            return tile
+
+        def load_weight(w, name, pieces):
+            rows = w.rearrange("(p j) c -> p j c", j=PACK)
+            width = w.shape[1] // pieces
+            tiles = []
+            for i in range(pieces):
+                tile = sb.tile([P, PACK, width], F32, name="%s_raw%d" % (name, i))
+                nc.sync.dma_start(tile[:], rows[:, :, i * width : (i + 1) * width])
+                tiles.append(tile)
+            return tiles
+
+        def round_weight(raws, name, on_vector):
+            grouped = sb.tile([P, PACK, P, PACK], BF16, name=name + "_bf", align_bytes=64)
+            width = P // len(raws)
+            for i, raw in enumerate(raws):
+                dst = grouped[:, :, i * width : (i + 1) * width, :].rearrange("p t m j -> p m j t")
+                src = raw[:].rearrange("p j (m t) -> p m j t", t=PACK)
+                if i in on_vector:
+                    nc.vector.tensor_copy(dst, src)
+                else:
+                    nc.scalar.activation(dst, src, COPY)
+            return grouped
+
+        def quantize(grouped_flat, name, pieces=1):
+            cols = grouped_flat.shape[1] // PACK
+            codes = sb.tile([P, cols], U32, name=name + "_codes", align_bytes=64)
+            scales = sb.tile([P, cols], U8, name=name + "_scales", align_bytes=64)
+            w = cols // pieces
+            for i in range(pieces):
+                nc.vector.quantize_mx(
+                    out=codes[:, i * w : (i + 1) * w].bitcast(FP8X4),
+                    scales=scales[:, i * w : (i + 1) * w],
+                    in_=grouped_flat[:, i * w * PACK : (i + 1) * w * PACK],
+                )
+            return codes, scales
+
+        def flat(tile):
+            return tile[:].rearrange("p a b c -> p (a b c)")
+
+        def mx(out, lhs, lhs_cols, rhs, rhs_cols, start, stop):
+            nc.tensor.matmul_mx(
+                out=out,
+                lhsT=lhs[0][:, lhs_cols].bitcast(FP8X4),
+                lhsT_scale=lhs[1][:, lhs_cols],
+                rhs=rhs[0][:, rhs_cols].bitcast(FP8X4),
+                rhs_scale=rhs[1][:, rhs_cols],
+                start=start,
+                stop=stop,
+            )
+
+        def pick(words, scales, lst, n, name):
+            codes = sb.tile([P, n], U32, name=name + "_codes", align_bytes=64)
+            plane = sb.tile([P, n], U8, name=name + "_scales", align_bytes=64)
+            nc.vector.tensor_copy(codes[:], words[:].indirect(lst[:]))
+            nc.vector.tensor_copy(plane[:], scales[:].indirect(lst[:]))
+            return codes, plane
+
+        def block(i):
+            return slice(i * P, (i + 1) * P)
+
+        offs_t = load_list(offs, "offs_t")
+        xw = load_words(x_words, "xw")
+        xs = load_scales(x_scales, "xs", nc.sync)
+        w1_raw = load_weight(w1, "w1", 2)
+        pos = [load_list(pos1, "pos1_t"), load_list(pos2, "pos2_t"), load_list(pos3, "pos3_t")]
+        usr_t = load_list(usr, "usr_t")
+        gates = sb.tile([P, D, V], F32, name="gates")
+        nc.sync.dma_start(gates[:], gate.rearrange("d p v -> p d v"))
+        ew = load_words(e_words, "ew")
+        es = load_scales(e_scales, "es", nc.gpsimd)
+        w2_raw = load_weight(w2, "w2", 2)
+        w3_raw = load_weight(w3, "w3", 2)
+        w4_raw = load_weight(w4, "w4", 2)
+
+        xq = pick(xw, xs, offs_t, S, "xq")
+        w1q = quantize(flat(round_weight(w1_raw, "w1", (1,))), "w1", 2)
+        h = []
+        for t in range(PACK):
+            bank = ps.tile([P, S], F32, name="bank%d" % t, tag="bank%d" % t)
+            mx(bank[:], w1q, block(t), xq, slice(0, S), True, True)
+            h_t = sb.tile([P, S], F32, name="h%d" % t)
+            nc.scalar.copy(h_t[:], bank[:])
+            h.append(h_t)
+        eq = pick(ew, es, usr_t, V, "eq")
+
+        def gather(half):
+            terms = [sb.tile([P, PACK, VH], F32, name="term%d_%d" % (half, d)) for d in range(D)]
+            for t in range(PACK):
+                for d in range(D):
+                    nc.vector.tensor_tensor(
+                        terms[d][:, t, :],
+                        h[t][:].indirect(pos[d][:, half * LIST_COLS : (half + 1) * LIST_COLS]),
+                        gates[:, d, block(half)],
+                        MULT,
+                    )
+            return terms
+
+        def by_line(ap):
+            return ap.rearrange("p t (c i) -> p c t i", i=4)
+
+        def by_line_out(ap):
+            return ap.rearrange("p (c i) t -> p c t i", i=4)
+
+        def combine(half, terms, gg):
+            part = sb.tile([P, PACK, VH], F32, name="part%d" % half)
+            z = sb.tile([P, PACK, VH], F32, name="z%d" % half)
+            zy = sb.tile([P, 2, VH, PACK], BF16, name="zy%d" % half, align_bytes=64)
+            nc.vector.tensor_tensor(part[:], terms[0][:], terms[1][:], ADD)
+            nc.vector.tensor_tensor(z[:], part[:], terms[2][:], ADD)
+            nc.scalar.copy(by_line_out(zy[:, 0]), by_line(z[:]))
+            nc.vector.tensor_tensor(by_line_out(zy[:, 1]), by_line(z[:]), by_line(gg[:]), MULT)
+            return zy
+
+        terms0 = gather(0)
+        w2q = quantize(flat(round_weight(w2_raw, "w2", ())), "w2")
+        gg = []
+        for half in range(HALVES):
+            bank = ps.tile([P, PACK, VH], F32, name="gg%d" % half)
+            for t in range(PACK):
+                mx(bank[:, t, :], w2q, block(t), eq, block(half), True, True)
+            gg.append(bank)
+        zy0 = combine(0, terms0, gg[0])
+        w3_bf = round_weight(w3_raw, "w3", ())
+        w4_bf = round_weight(w4_raw, "w4", ())
+        terms1 = gather(1)
+        zyq0 = quantize(flat(zy0), "zy0")
+        w3q = quantize(flat(w3_bf), "w3")
+        w4q = quantize(flat(w4_bf), "w4")
+
+        out_rows = out_0.rearrange("(p t) v -> p t v", t=PACK)
+        out_words = out_1[0].rearrange("p c r -> p (c r)").bitcast(I32)
+        out_scales = sb.tile([P, V], U8, name="out_scales", align_bytes=64)
+
+        def finish(half, zyq, round_on_vector):
+            res = sb.tile([P, PACK, VH], F32, name="res%d" % half)
+            for t in range(PACK):
+                bank = ps.tile([P, VH], F32, name="res_bank%d_%d" % (half, t), tag="bank%d" % t)
+                mx(bank[:], w3q, block(t), zyq, block(0), True, False)
+                mx(bank[:], w4q, block(t), zyq, block(1), False, True)
+                nc.scalar.activation(res[:, t, :], bank[:], RELU)
+            nc.sync.dma_start(out_rows[:, :, block(half)], res[:])
+            res_bf = sb.tile([P, VH, PACK], BF16, name="res_bf%d" % half, align_bytes=64)
+            if round_on_vector:
+                nc.vector.tensor_copy(by_line_out(res_bf[:]), by_line(res[:]))
+            else:
+                nc.scalar.copy(by_line_out(res_bf[:]), by_line(res[:]))
+            return res_bf
+
+        def hand_on(half, res_bf):
+            codes = sb.tile([P, VH], U32, name="out_codes%d" % half, align_bytes=64)
+            nc.vector.quantize_mx(
+                out=codes[:].bitcast(FP8X4),
+                scales=out_scales[:, block(half)],
+                in_=res_bf[:].rearrange("p v t -> p (v t)"),
+            )
+            nc.sync.dma_start(out_words[:, block(half)], codes[:].bitcast(I32))
+
+        res_bf0 = finish(0, zyq0, False)
+        zy1 = combine(1, terms1, gg[1])
+        zyq1 = quantize(flat(zy1), "zy1")
+        hand_on(0, res_bf0)
+        res_bf1 = finish(1, zyq1, True)
+        hand_on(1, res_bf1)
+        for q in range(4):
+            queue = nc.scalar if q % 2 else nc.sync
+            queue.dma_start(
+                out_2[0, 4 * q : 4 * q + 4, :].bitcast(I32), out_scales[32 * q : 32 * q + 4, :].bitcast(I32)
+            )

@@ -44,9 +44,11 @@ def tile_picked_yngcf_relu_po_kernel(
 
         def load_scales(src, name, queue):
             tile = sb.tile([P, T], U8, name=name, align_bytes=64)
-            nc.vector.memset(tile[:].bitcast(I32), 0)
             for q in range(4):
-                queue.dma_start(tile[32 * q : 32 * q + 4, :].bitcast(I32), src[0, 4 * q : 4 * q + 4, :].bitcast(I32))
+                rows = src[0, 4 * q : 4 * q + 4, :].bitcast(I32)
+                queue.dma_start(
+                    tile[32 * q : 32 * q + 32, :].bitcast(I32), rows.unsqueeze(0).broadcast_to([8, 4, T // 4])
+                )
             return tile
 
         def load_weight(w, name, pieces):
@@ -60,7 +62,7 @@ def tile_picked_yngcf_relu_po_kernel(
             return tiles
 
         def round_weight(raws, name, on_vector):
-            grouped = sb.tile([P, PACK, P, PACK], BF16, name=name + "_bf", align_bytes=64)
+            grouped = sb.tile([P, PACK, P, PACK], BF16, name=name + "_bf", tag=name + "_bf", align_bytes=64)
             width = P // len(raws)
             for i, raw in enumerate(raws):
                 dst = grouped[:, :, i * width : (i + 1) * width, :].rearrange("p t m j -> p m j t")
@@ -98,32 +100,35 @@ def tile_picked_yngcf_relu_po_kernel(
                 stop=stop,
             )
 
-        def pick(words, scales, lst, n, name):
-            codes = sb.tile([P, n], U32, name=name + "_codes", align_bytes=64)
-            plane = sb.tile([P, n], U8, name=name + "_scales", align_bytes=64)
-            nc.vector.tensor_copy(codes[:], words[:].indirect(lst[:]))
-            nc.vector.tensor_copy(plane[:], scales[:].indirect(lst[:]))
-            return codes, plane
+        def pick(table, lst, n, dtype, name):
+            picked = sb.tile([P, n], dtype, name=name, align_bytes=64)
+            nc.vector.tensor_copy(picked[:], table[:].indirect(lst[:]))
+            return picked
 
         def block(i):
             return slice(i * P, (i + 1) * P)
+
+        def load_gates(half):
+            tile = sb.tile([P, D, VH], F32, name="gates%d" % half)
+            nc.sync.dma_start(tile[:], gate.rearrange("d p v -> p d v")[:, :, block(half)])
+            return tile
 
         offs_t = load_list(offs, "offs_t")
         xw = load_words(x_words, "xw")
         xs = load_scales(x_scales, "xs", nc.sync)
         w1_raw = load_weight(w1, "w1", 2)
-        pos = [load_list(pos1, "pos1_t"), load_list(pos2, "pos2_t"), load_list(pos3, "pos3_t")]
         usr_t = load_list(usr, "usr_t")
-        gates = sb.tile([P, D, V], F32, name="gates")
-        nc.sync.dma_start(gates[:], gate.rearrange("d p v -> p d v"))
         ew = load_words(e_words, "ew")
-        es = load_scales(e_scales, "es", nc.gpsimd)
+        pos = [load_list(pos1, "pos1_t"), load_list(pos2, "pos2_t"), load_list(pos3, "pos3_t")]
+        gates = [load_gates(0)]
+        es = load_scales(e_scales, "es", nc.sync)
+        gates.append(load_gates(1))
         w2_raw = load_weight(w2, "w2", 2)
         w3_raw = load_weight(w3, "w3", 2)
         w4_raw = load_weight(w4, "w4", 2)
 
-        xq = pick(xw, xs, offs_t, S, "xq")
-        w1q = quantize(flat(round_weight(w1_raw, "w1", (1,))), "w1", 2)
+        xq = (pick(xw, offs_t, S, U32, "xq_codes"), pick(xs, offs_t, S, U8, "xq_scales"))
+        w1q = quantize(flat(round_weight(w1_raw, "w1", (1,))), "w1", 4)
         h = []
         for t in range(PACK):
             bank = ps.tile([P, S], F32, name="bank%d" % t, tag="bank%d" % t)
@@ -131,16 +136,16 @@ def tile_picked_yngcf_relu_po_kernel(
             h_t = sb.tile([P, S], F32, name="h%d" % t)
             nc.scalar.copy(h_t[:], bank[:])
             h.append(h_t)
-        eq = pick(ew, es, usr_t, V, "eq")
+        eq_codes = pick(ew, usr_t, V, U32, "eq_codes")
 
         def gather(half):
-            terms = [sb.tile([P, PACK, VH], F32, name="term%d_%d" % (half, d)) for d in range(D)]
+            terms = [sb.tile([P, PACK, VH], F32, name="term%d_%d" % (half, d), tag="term%d" % d) for d in range(D)]
             for t in range(PACK):
                 for d in range(D):
                     nc.vector.tensor_tensor(
                         terms[d][:, t, :],
                         h[t][:].indirect(pos[d][:, half * LIST_COLS : (half + 1) * LIST_COLS]),
-                        gates[:, d, block(half)],
+                        gates[half][:, d, :],
                         MULT,
                     )
             return terms
@@ -151,17 +156,21 @@ def tile_picked_yngcf_relu_po_kernel(
         def by_line_out(ap):
             return ap.rearrange("p (c i) t -> p c t i", i=4)
 
-        def combine(half, terms, gg):
-            part = sb.tile([P, PACK, VH], F32, name="part%d" % half)
-            z = sb.tile([P, PACK, VH], F32, name="z%d" % half)
-            zy = sb.tile([P, 2, VH, PACK], BF16, name="zy%d" % half, align_bytes=64)
+        def combine(half, terms, gg, part_tag, z_tag):
+            part = sb.tile([P, PACK, VH], F32, name="part%d" % half, tag=part_tag, align_bytes=64)
+            z = sb.tile([P, PACK, VH], F32, name="z%d" % half, tag=z_tag, align_bytes=64)
+            z_bf = sb.tile([P, VH, PACK], BF16, name="z_bf%d" % half, align_bytes=64)
+            y_bf = sb.tile([P, VH, PACK], BF16, name="y_bf%d" % half, align_bytes=64)
             nc.vector.tensor_tensor(part[:], terms[0][:], terms[1][:], ADD)
             nc.vector.tensor_tensor(z[:], part[:], terms[2][:], ADD)
-            nc.scalar.copy(by_line_out(zy[:, 0]), by_line(z[:]))
-            nc.vector.tensor_tensor(by_line_out(zy[:, 1]), by_line(z[:]), by_line(gg[:]), MULT)
-            return zy
+            nc.scalar.copy(by_line_out(z_bf[:]), by_line(z[:]))
+            nc.vector.tensor_tensor(by_line_out(y_bf[:]), by_line(z[:]), by_line(gg[:]), MULT)
+            zq = quantize(z_bf[:].rearrange("p v t -> p (v t)"), "z%d" % half)
+            yq = quantize(y_bf[:].rearrange("p v t -> p (v t)"), "y%d" % half)
+            return zq, yq
 
         terms0 = gather(0)
+        eq = (eq_codes, pick(es, usr_t, V, U8, "eq_scales"))
         w2q = quantize(flat(round_weight(w2_raw, "w2", ())), "w2")
         gg = []
         for half in range(HALVES):
@@ -169,11 +178,10 @@ def tile_picked_yngcf_relu_po_kernel(
             for t in range(PACK):
                 mx(bank[:, t, :], w2q, block(t), eq, block(half), True, True)
             gg.append(bank)
-        zy0 = combine(0, terms0, gg[0])
         w3_bf = round_weight(w3_raw, "w3", ())
+        zyq0 = combine(0, terms0, gg[0], "part0", "w2_bf")
         w4_bf = round_weight(w4_raw, "w4", ())
         terms1 = gather(1)
-        zyq0 = quantize(flat(zy0), "zy0")
         w3q = quantize(flat(w3_bf), "w3")
         w4q = quantize(flat(w4_bf), "w4")
 
@@ -181,22 +189,20 @@ def tile_picked_yngcf_relu_po_kernel(
         out_words = out_1[0].rearrange("p c r -> p (c r)").bitcast(I32)
         out_scales = sb.tile([P, V], U8, name="out_scales", align_bytes=64)
 
-        def finish(half, zyq, round_on_vector):
+        def finish(half, zq, yq):
             res = sb.tile([P, PACK, VH], F32, name="res%d" % half)
+            banks = [ps.tile([P, VH], F32, name="res_bank%d_%d" % (half, t), tag="bank%d" % t) for t in range(PACK)]
             for t in range(PACK):
-                bank = ps.tile([P, VH], F32, name="res_bank%d_%d" % (half, t), tag="bank%d" % t)
-                mx(bank[:], w3q, block(t), zyq, block(0), True, False)
-                mx(bank[:], w4q, block(t), zyq, block(1), False, True)
-                nc.scalar.activation(res[:, t, :], bank[:], RELU)
+                mx(banks[t][:], w3q, block(t), zq, block(0), True, False)
+            for t in range(PACK):
+                mx(banks[t][:], w4q, block(t), yq, block(0), False, True)
+                nc.scalar.activation(res[:, t, :], banks[t][:], RELU)
             nc.sync.dma_start(out_rows[:, :, block(half)], res[:])
-            res_bf = sb.tile([P, VH, PACK], BF16, name="res_bf%d" % half, align_bytes=64)
-            if round_on_vector:
-                nc.vector.tensor_copy(by_line_out(res_bf[:]), by_line(res[:]))
-            else:
-                nc.scalar.copy(by_line_out(res_bf[:]), by_line(res[:]))
-            return res_bf
+            return res
 
-        def hand_on(half, res_bf):
+        def hand_on(half, res):
+            res_bf = sb.tile([P, VH, PACK], BF16, name="res_bf%d" % half, align_bytes=64)
+            nc.vector.tensor_copy(by_line_out(res_bf[:]), by_line(res[:]))
             codes = sb.tile([P, VH], U32, name="out_codes%d" % half, align_bytes=64)
             nc.vector.quantize_mx(
                 out=codes[:].bitcast(FP8X4),
@@ -205,12 +211,11 @@ def tile_picked_yngcf_relu_po_kernel(
             )
             nc.sync.dma_start(out_words[:, block(half)], codes[:].bitcast(I32))
 
-        res_bf0 = finish(0, zyq0, False)
-        zy1 = combine(1, terms1, gg[1])
-        zyq1 = quantize(flat(zy1), "zy1")
-        hand_on(0, res_bf0)
-        res_bf1 = finish(1, zyq1, True)
-        hand_on(1, res_bf1)
+        res0 = finish(0, *zyq0)
+        zyq1 = combine(1, terms1, gg[1], "w4_bf", "z1")
+        hand_on(0, res0)
+        res1 = finish(1, *zyq1)
+        hand_on(1, res1)
         for q in range(4):
             queue = nc.scalar if q % 2 else nc.sync
             queue.dma_start(

@@ -65,8 +65,8 @@ def tile_picked_yngcf_relu_po_kernel(
             grouped = sb.tile([P, PACK, P, PACK], BF16, name=name + "_bf", tag=name + "_bf", align_bytes=64)
             width = P // len(raws)
             for i, raw in enumerate(raws):
-                dst = grouped[:, :, i * width : (i + 1) * width, :].rearrange("p t m j -> p m j t")
-                src = raw[:].rearrange("p j (m t) -> p m j t", t=PACK)
+                dst = grouped[:, :, i * width : (i + 1) * width, :].rearrange("p t m j -> p m t j")
+                src = raw[:].rearrange("p j (m t) -> p m t j", t=PACK)
                 if i in on_vector:
                     nc.vector.tensor_copy(dst, src)
                 else:
@@ -123,9 +123,9 @@ def tile_picked_yngcf_relu_po_kernel(
         gates = [load_gates(0)]
         es = load_scales(e_scales, "es", nc.sync)
         gates.append(load_gates(1))
-        w2_raw = load_weight(w2, "w2", 2)
-        w3_raw = load_weight(w3, "w3", 2)
-        w4_raw = load_weight(w4, "w4", 2)
+        w2_raw = load_weight(w2, "w2", 1)
+        w3_raw = load_weight(w3, "w3", 1)
+        w4_raw = load_weight(w4, "w4", 1)
 
         xq = (pick(xw, offs_t, S, U32, "xq_codes"), pick(xs, offs_t, S, U8, "xq_scales"))
         w1q = quantize(flat(round_weight(w1_raw, "w1", (1,))), "w1", 4)
@@ -156,11 +156,11 @@ def tile_picked_yngcf_relu_po_kernel(
         def by_line_out(ap):
             return ap.rearrange("p (c i) t -> p c t i", i=4)
 
-        def combine(half, terms, gg, part_tag, z_tag):
-            part = sb.tile([P, PACK, VH], F32, name="part%d" % half, tag=part_tag, align_bytes=64)
+        def combine(half, terms, gg, z_tag, y_tag):
+            part = sb.tile([P, PACK, VH], F32, name="part%d" % half)
             z = sb.tile([P, PACK, VH], F32, name="z%d" % half, tag=z_tag, align_bytes=64)
             z_bf = sb.tile([P, VH, PACK], BF16, name="z_bf%d" % half, align_bytes=64)
-            y_bf = sb.tile([P, VH, PACK], BF16, name="y_bf%d" % half, align_bytes=64)
+            y_bf = sb.tile([P, VH, PACK], BF16, name="y_bf%d" % half, tag=y_tag, align_bytes=64)
             nc.vector.tensor_tensor(part[:], terms[0][:], terms[1][:], ADD)
             nc.vector.tensor_tensor(z[:], part[:], terms[2][:], ADD)
             nc.scalar.copy(by_line_out(z_bf[:]), by_line(z[:]))
@@ -179,7 +179,7 @@ def tile_picked_yngcf_relu_po_kernel(
                 mx(bank[:, t, :], w2q, block(t), eq, block(half), True, True)
             gg.append(bank)
         w3_bf = round_weight(w3_raw, "w3", ())
-        zyq0 = combine(0, terms0, gg[0], "part0", "w2_bf")
+        zyq0 = combine(0, terms0, gg[0], "w2_bf", "y_bf0")
         w4_bf = round_weight(w4_raw, "w4", ())
         terms1 = gather(1)
         w3q = quantize(flat(w3_bf), "w3")
@@ -212,7 +212,7 @@ def tile_picked_yngcf_relu_po_kernel(
             nc.sync.dma_start(out_words[:, block(half)], codes[:].bitcast(I32))
 
         res0 = finish(0, *zyq0)
-        zyq1 = combine(1, terms1, gg[1], "w4_bf", "z1")
+        zyq1 = combine(1, terms1, gg[1], "z1", "w4_bf")
         hand_on(0, res0)
         res1 = finish(1, *zyq1)
         hand_on(1, res1)

@@ -2,7 +2,7 @@ from contextlib import ExitStack
 
 import concourse.mybir as mybir
 
-K, T, S, V, H, N, D = 512, 1024, 512, 256, 512, 512, 3
+K, T, S, V, H, N = 512, 1024, 512, 256, 512, 512
 FLOPS = 2 * K * H * S + 2 * K * H * V + 2 * 2 * H * N * V
 
 F32 = mybir.dt.float32
@@ -19,9 +19,10 @@ RELU = mybir.ActivationFunctionType.Relu
 
 P = 128
 PACK = 4
+QUADRANTS = 4
 VH = 128
 HALVES = V // VH
-LIST_COLS = VH // 16
+W1_SCALAR_COLS = 96
 
 
 def tile_picked_yngcf_relu_po_kernel(
@@ -31,6 +32,9 @@ def tile_picked_yngcf_relu_po_kernel(
     with ExitStack() as ctx:
         sb = ctx.enter_context(tc.tile_pool(name="sb", bufs=1))
         ps = ctx.enter_context(tc.psum_pool(name="ps", bufs=1))
+
+        def block(i):
+            return slice(i * P, (i + 1) * P)
 
         def load_list(src, name):
             tile = sb.tile(list(src.shape), U16, name=name)
@@ -42,52 +46,53 @@ def tile_picked_yngcf_relu_po_kernel(
             nc.sync.dma_start(tile[:].bitcast(I32), src[0].rearrange("p c r -> p (c r)").bitcast(I32))
             return tile
 
-        def load_scales(src, name, queue):
+        def load_scales(src, name):
             tile = sb.tile([P, T], U8, name=name, align_bytes=64)
-            for q in range(4):
-                rows = src[0, 4 * q : 4 * q + 4, :].bitcast(I32)
-                queue.dma_start(
-                    tile[32 * q : 32 * q + 32, :].bitcast(I32), rows.unsqueeze(0).broadcast_to([8, 4, T // 4])
+            nc.vector.memset(tile[:].bitcast(I32), 0)
+            for q in range(QUADRANTS):
+                nc.sync.dma_start(
+                    tile[32 * q : 32 * q + 4, :].bitcast(I32), src[0, 4 * q : 4 * q + 4, :].bitcast(I32)
                 )
             return tile
 
-        def load_weight(w, name, pieces):
-            rows = w.rearrange("(p j) c -> p j c", j=PACK)
-            width = w.shape[1] // pieces
-            tiles = []
-            for i in range(pieces):
-                tile = sb.tile([P, PACK, width], F32, name="%s_raw%d" % (name, i))
-                nc.sync.dma_start(tile[:], rows[:, :, i * width : (i + 1) * width])
-                tiles.append(tile)
-            return tiles
+        def load_weight(w, name, c0, c1):
+            tile = sb.tile([P, PACK, c1 - c0], F32, name=name + "_raw", tag=name + "_raw", align_bytes=64)
+            nc.sync.dma_start(tile[:], w.rearrange("(p j) c -> p j c", j=PACK)[:, :, c0:c1])
+            return tile
 
-        def round_weight(raws, name, on_vector):
-            grouped = sb.tile([P, PACK, P, PACK], BF16, name=name + "_bf", tag=name + "_bf", align_bytes=64)
-            width = P // len(raws)
-            for i, raw in enumerate(raws):
-                dst = grouped[:, :, i * width : (i + 1) * width, :].rearrange("p t m j -> p m t j")
-                src = raw[:].rearrange("p j (m t) -> p m t j", t=PACK)
-                if i in on_vector:
-                    nc.vector.tensor_copy(dst, src)
-                else:
-                    nc.scalar.activation(dst, src, COPY)
-            return grouped
+        def load_gate(d):
+            tile = sb.tile([P, V], F32, name="gate%d" % d)
+            nc.sync.dma_start(tile[:], gate[d])
+            return tile
 
-        def quantize(grouped_flat, name, pieces=1):
-            cols = grouped_flat.shape[1] // PACK
+        def scalar_copy(dst, src):
+            nc.scalar.activation(dst, src, COPY)
+
+        def round_weight(name, shares):
+            dealt = sb.tile([P, PACK, P, PACK], BF16, name=name + "_bf", tag=name + "_bf", align_bytes=64)
+            m0 = 0
+            for copy, raw in shares:
+                m1 = m0 + raw.shape[2] // PACK
+                copy(
+                    dealt[:, :, m0:m1, :].rearrange("p t m j -> p m t j"),
+                    raw.rearrange("p j (m t) -> p m t j", t=PACK),
+                )
+                m0 = m1
+            return dealt[:].rearrange("p t m j -> p (t m) j")
+
+        def quantize(grouped, name, pieces=1):
+            cols = grouped.shape[1]
             codes = sb.tile([P, cols], U32, name=name + "_codes", align_bytes=64)
             scales = sb.tile([P, cols], U8, name=name + "_scales", align_bytes=64)
-            w = cols // pieces
+            width = cols // pieces
             for i in range(pieces):
+                piece = slice(i * width, (i + 1) * width)
                 nc.vector.quantize_mx(
-                    out=codes[:, i * w : (i + 1) * w].bitcast(FP8X4),
-                    scales=scales[:, i * w : (i + 1) * w],
-                    in_=grouped_flat[:, i * w * PACK : (i + 1) * w * PACK],
+                    out=codes[:, piece].bitcast(FP8X4),
+                    scales=scales[:, piece],
+                    in_=grouped[:, piece, :].rearrange("p c j -> p (c j)"),
                 )
             return codes, scales
-
-        def flat(tile):
-            return tile[:].rearrange("p a b c -> p (a b c)")
 
         def mx(out, lhs, lhs_cols, rhs, rhs_cols, start, stop):
             nc.tensor.matmul_mx(
@@ -100,109 +105,118 @@ def tile_picked_yngcf_relu_po_kernel(
                 stop=stop,
             )
 
-        def pick(table, lst, n, dtype, name):
-            picked = sb.tile([P, n], dtype, name=name, align_bytes=64)
-            nc.vector.tensor_copy(picked[:], table[:].indirect(lst[:]))
+        def pick(table, offsets, count, dtype, name):
+            picked = sb.tile([P, count], dtype, name=name, align_bytes=64)
+            nc.vector.tensor_copy(picked[:], table[:].indirect(offsets[:]))
             return picked
 
-        def block(i):
-            return slice(i * P, (i + 1) * P)
+        def tiles_view(ap):
+            return ap.rearrange("p t (c i) -> p c t i", i=2)
 
-        def load_gates(half):
-            tile = sb.tile([P, D, VH], F32, name="gates%d" % half)
-            nc.sync.dma_start(tile[:], gate.rearrange("d p v -> p d v")[:, :, block(half)])
-            return tile
+        def interleaved_view(ap):
+            return ap.rearrange("p (c i) t -> p c t i", i=2)
 
         offs_t = load_list(offs, "offs_t")
+        w1_left = load_weight(w1, "w1_left", 0, H // 2)
+        xs = load_scales(x_scales, "xs")
         xw = load_words(x_words, "xw")
-        xs = load_scales(x_scales, "xs", nc.sync)
-        w1_raw = load_weight(w1, "w1", 2)
+        w1_right = load_weight(w1, "w1_right", H // 2, H)
         usr_t = load_list(usr, "usr_t")
         ew = load_words(e_words, "ew")
-        pos = [load_list(pos1, "pos1_t"), load_list(pos2, "pos2_t"), load_list(pos3, "pos3_t")]
-        gates = [load_gates(0)]
-        es = load_scales(e_scales, "es", nc.sync)
-        gates.append(load_gates(1))
-        w2_raw = load_weight(w2, "w2", 1)
-        w3_raw = load_weight(w3, "w3", 1)
-        w4_raw = load_weight(w4, "w4", 1)
+        pos, gates = [], []
+        for d, src in enumerate((pos1, pos2)):
+            pos.append(load_list(src, "pos%d_t" % d))
+            gates.append(load_gate(d))
+        w2_raw = load_weight(w2, "w2", 0, H)
+        pos.append(load_list(pos3, "pos2_t"))
+        gates.append(load_gate(2))
+        es = load_scales(e_scales, "es")
+        w3_raw = load_weight(w3, "w3", 0, N)
+        w4_raw = load_weight(w4, "w4", 0, N)
 
-        xq = (pick(xw, offs_t, S, U32, "xq_codes"), pick(xs, offs_t, S, U8, "xq_scales"))
-        w1q = quantize(flat(round_weight(w1_raw, "w1", (1,))), "w1", 4)
-        h = []
-        for t in range(PACK):
-            bank = ps.tile([P, S], F32, name="bank%d" % t, tag="bank%d" % t)
-            mx(bank[:], w1q, block(t), xq, slice(0, S), True, True)
-            h_t = sb.tile([P, S], F32, name="h%d" % t)
-            nc.scalar.copy(h_t[:], bank[:])
-            h.append(h_t)
+        xq_scales = pick(xs, offs_t, S, U8, "xq_scales")
+        xq = (pick(xw, offs_t, S, U32, "xq_codes"), xq_scales)
+        w1_shares = [
+            (scalar_copy, w1_left[:]),
+            (scalar_copy, w1_right[:, :, :W1_SCALAR_COLS]),
+            (nc.vector.tensor_copy, w1_right[:, :, W1_SCALAR_COLS:]),
+        ]
+        w1q = quantize(round_weight("w1", w1_shares), "w1", PACK)
+        h = [sb.tile([P, S], F32, name="h%d" % t) for t in range(PACK)]
+        passes = [(0, slice(0, S // 2), "bank4"), (0, slice(S // 2, S), "bank0")]
+        passes.extend((t, slice(0, S), "bank%d" % t) for t in range(1, PACK))
+        for t, cols, tag in passes:
+            bank = ps.tile([P, cols.stop - cols.start], F32, name="h_" + tag, tag=tag)
+            mx(bank[:], w1q, block(t), xq, cols, True, True)
+            nc.scalar.copy(h[t][:, cols], bank[:])
         eq_codes = pick(ew, usr_t, V, U32, "eq_codes")
 
-        def gather(half):
-            terms = [sb.tile([P, PACK, VH], F32, name="term%d_%d" % (half, d), tag="term%d" % d) for d in range(D)]
-            for t in range(PACK):
-                for d in range(D):
-                    nc.vector.tensor_tensor(
-                        terms[d][:, t, :],
-                        h[t][:].indirect(pos[d][:, half * LIST_COLS : (half + 1) * LIST_COLS]),
-                        gates[half][:, d, :],
-                        MULT,
-                    )
-            return terms
+        def gather(term, t, d):
+            nc.vector.tensor_tensor(term[:, t, :], h[t][:].indirect(pos[d][:]), gates[d][:], MULT)
 
-        def by_line(ap):
-            return ap.rearrange("p t (c i) -> p c t i", i=4)
-
-        def by_line_out(ap):
-            return ap.rearrange("p (c i) t -> p c t i", i=4)
-
-        def combine(half, terms, gg, z_tag, y_tag):
-            part = sb.tile([P, PACK, VH], F32, name="part%d" % half)
-            z = sb.tile([P, PACK, VH], F32, name="z%d" % half, tag=z_tag, align_bytes=64)
-            z_bf = sb.tile([P, VH, PACK], BF16, name="z_bf%d" % half, align_bytes=64)
-            y_bf = sb.tile([P, VH, PACK], BF16, name="y_bf%d" % half, tag=y_tag, align_bytes=64)
-            nc.vector.tensor_tensor(part[:], terms[0][:], terms[1][:], ADD)
-            nc.vector.tensor_tensor(z[:], part[:], terms[2][:], ADD)
-            nc.scalar.copy(by_line_out(z_bf[:]), by_line(z[:]))
-            nc.vector.tensor_tensor(by_line_out(y_bf[:]), by_line(z[:]), by_line(gg[:]), MULT)
-            zq = quantize(z_bf[:].rearrange("p v t -> p (v t)"), "z%d" % half)
-            yq = quantize(y_bf[:].rearrange("p v t -> p (v t)"), "y%d" % half)
-            return zq, yq
-
-        terms0 = gather(0)
+        terms = [sb.tile([P, PACK, V], F32, name="term%d" % d) for d in range(2)]
+        for t in range(PACK):
+            for d in range(2):
+                gather(terms[d], t, d)
         eq = (eq_codes, pick(es, usr_t, V, U8, "eq_scales"))
-        w2q = quantize(flat(round_weight(w2_raw, "w2", ())), "w2")
+        part = sb.tile([P, PACK, V], F32, name="part")
+        nc.vector.tensor_tensor(part[:], terms[0][:], terms[1][:], ADD)
+
+        w2q = quantize(round_weight("w2", [(scalar_copy, w2_raw[:])]), "w2")
         gg = []
         for half in range(HALVES):
-            bank = ps.tile([P, PACK, VH], F32, name="gg%d" % half)
+            bank = ps.tile([P, PACK, VH], F32, name="gg%d" % half, tag="gg%d" % half)
             for t in range(PACK):
                 mx(bank[:, t, :], w2q, block(t), eq, block(half), True, True)
             gg.append(bank)
-        w3_bf = round_weight(w3_raw, "w3", ())
-        zyq0 = combine(0, terms0, gg[0], "w2_bf", "y_bf0")
-        w4_bf = round_weight(w4_raw, "w4", ())
-        terms1 = gather(1)
-        w3q = quantize(flat(w3_bf), "w3")
-        w4q = quantize(flat(w4_bf), "w4")
+
+        last = sb.tile([P, PACK, V], F32, name="term2", tag="w2_bf", align_bytes=64)
+        for t in range(PACK):
+            gather(last, t, 2)
+        w3q = quantize(round_weight("w3", [(scalar_copy, w3_raw[:])]), "w3")
+        w4_bf = round_weight("w4", [(scalar_copy, w4_raw[:])])
+
+        z = sb.tile([P, HALVES, PACK, VH], F32, name="z", tag="w4_raw", align_bytes=64)
+
+        def add_last(half):
+            nc.vector.tensor_tensor(z[:, half], part[:, :, block(half)], last[:, :, block(half)], ADD)
+            z_bf = sb.tile([P, VH, PACK], BF16, name="z_bf%d" % half, align_bytes=64)
+            nc.scalar.copy(interleaved_view(z_bf[:]), tiles_view(z[:, half]))
+            return z_bf
+
+        def times_gg(half):
+            y_bf = sb.tile([P, VH, PACK], BF16, name="y_bf%d" % half, align_bytes=64)
+            nc.vector.tensor_tensor(interleaved_view(y_bf[:]), tiles_view(z[:, half]), tiles_view(gg[half][:]), MULT)
+            return y_bf
+
+        z_bf0 = add_last(0)
+        w4q = quantize(w4_bf, "w4")
+        zq0 = quantize(z_bf0[:], "z0")
+        y_bf0 = times_gg(0)
+        z_bf1 = add_last(1)
+        yq0 = quantize(y_bf0[:], "y0")
+        y_bf1 = times_gg(1)
+        zq1 = quantize(z_bf1[:], "z1")
+        yq1 = quantize(y_bf1[:], "y1")
 
         out_rows = out_0.rearrange("(p t) v -> p t v", t=PACK)
         out_words = out_1[0].rearrange("p c r -> p (c r)").bitcast(I32)
         out_scales = sb.tile([P, V], U8, name="out_scales", align_bytes=64)
 
-        def finish(half, zq, yq):
+        def finish(half, zq, yq, tags):
             res = sb.tile([P, PACK, VH], F32, name="res%d" % half)
-            banks = [ps.tile([P, VH], F32, name="res_bank%d_%d" % (half, t), tag="bank%d" % t) for t in range(PACK)]
+            banks = [ps.tile([P, VH], F32, name="res_bank%d_%d" % (half, t), tag=tags[t]) for t in range(PACK)]
             for t in range(PACK):
-                mx(banks[t][:], w3q, block(t), zq, block(0), True, False)
+                mx(banks[t][:], w3q, block(t), zq, slice(0, VH), True, False)
             for t in range(PACK):
-                mx(banks[t][:], w4q, block(t), yq, block(0), False, True)
+                mx(banks[t][:], w4q, block(t), yq, slice(0, VH), False, True)
                 nc.scalar.activation(res[:, t, :], banks[t][:], RELU)
             nc.sync.dma_start(out_rows[:, :, block(half)], res[:])
             return res
 
         def hand_on(half, res):
             res_bf = sb.tile([P, VH, PACK], BF16, name="res_bf%d" % half, align_bytes=64)
-            nc.vector.tensor_copy(by_line_out(res_bf[:]), by_line(res[:]))
+            nc.vector.tensor_copy(interleaved_view(res_bf[:]), tiles_view(res[:]))
             codes = sb.tile([P, VH], U32, name="out_codes%d" % half, align_bytes=64)
             nc.vector.quantize_mx(
                 out=codes[:].bitcast(FP8X4),
@@ -211,12 +225,11 @@ def tile_picked_yngcf_relu_po_kernel(
             )
             nc.sync.dma_start(out_words[:, block(half)], codes[:].bitcast(I32))
 
-        res0 = finish(0, *zyq0)
-        zyq1 = combine(1, terms1, gg[1], "z1", "w4_bf")
+        res0 = finish(0, zq0, yq0, ["bank0", "bank1", "bank2", "bank3"])
+        res1 = finish(1, zq1, yq1, ["bank4", "bank5", "gg0", "gg1"])
         hand_on(0, res0)
-        res1 = finish(1, *zyq1)
         hand_on(1, res1)
-        for q in range(4):
+        for q in range(QUADRANTS):
             queue = nc.scalar if q % 2 else nc.sync
             queue.dma_start(
                 out_2[0, 4 * q : 4 * q + 4, :].bitcast(I32), out_scales[32 * q : 32 * q + 4, :].bitcast(I32)

from contextlib import ExitStack

import concourse.mybir as mybir

K, T, S, V, H, N = 512, 1024, 512, 256, 512, 512
FLOPS = 2 * K * H * S + 2 * K * H * V + 2 * 2 * H * N * V

F32 = mybir.dt.float32
BF16 = mybir.dt.bfloat16
I32 = mybir.dt.int32
U32 = mybir.dt.uint32
U16 = mybir.dt.uint16
U8 = mybir.dt.uint8
FP8X4 = mybir.dt.float8_e4m3fn_x4
MULT = mybir.AluOpType.mult
ADD = mybir.AluOpType.add
COPY = mybir.ActivationFunctionType.Copy
RELU = mybir.ActivationFunctionType.Relu

P = 128
PACK = 4
QUADRANTS = 4
VH = 128
HALVES = V // VH
W1_SCALAR_COLS = 96


def tile_picked_yngcf_relu_po_kernel(
    tc, x_words, x_scales, e_words, e_scales, w1, w2, w3, w4, gate, offs, usr, pos1, pos2, pos3, out_0, out_1, out_2
):
    nc = tc.nc
    with ExitStack() as ctx:
        sb = ctx.enter_context(tc.tile_pool(name="sb", bufs=1))
        ps = ctx.enter_context(tc.psum_pool(name="ps", bufs=1))

        def block(i):
            return slice(i * P, (i + 1) * P)

        def load_list(src, name):
            tile = sb.tile(list(src.shape), U16, name=name)
            nc.sync.dma_start(tile[:], src)
            return tile

        def load_words(src, name):
            tile = sb.tile([P, T], U32, name=name, align_bytes=64)
            nc.sync.dma_start(tile[:].bitcast(I32), src[0].rearrange("p c r -> p (c r)").bitcast(I32))
            return tile

        def load_scales(src, name):
            tile = sb.tile([P, T], U8, name=name, align_bytes=64)
            nc.vector.memset(tile[:].bitcast(I32), 0)
            for q in range(QUADRANTS):
                nc.sync.dma_start(
                    tile[32 * q : 32 * q + 4, :].bitcast(I32), src[0, 4 * q : 4 * q + 4, :].bitcast(I32)
                )
            return tile

        def load_weight(w, name, c0, c1):
            tile = sb.tile([P, PACK, c1 - c0], F32, name=name + "_raw", tag=name + "_raw", align_bytes=64)
            nc.sync.dma_start(tile[:], w.rearrange("(p j) c -> p j c", j=PACK)[:, :, c0:c1])
            return tile

        def load_gate(d):
            tile = sb.tile([P, V], F32, name="gate%d" % d)
            nc.sync.dma_start(tile[:], gate[d])
            return tile

        def scalar_copy(dst, src):
            nc.scalar.activation(dst, src, COPY)

        def round_weight(name, shares):
            dealt = sb.tile([P, PACK, P, PACK], BF16, name=name + "_bf", tag=name + "_bf", align_bytes=64)
            m0 = 0
            for copy, raw in shares:
                m1 = m0 + raw.shape[2] // PACK
                copy(
                    dealt[:, :, m0:m1, :].rearrange("p t m j -> p m t j"),
                    raw.rearrange("p j (m t) -> p m t j", t=PACK),
                )
                m0 = m1
            return dealt[:].rearrange("p t m j -> p (t m) j")

        def quantize(grouped, name, pieces=1):
            cols = grouped.shape[1]
            codes = sb.tile([P, cols], U32, name=name + "_codes", align_bytes=64)
            scales = sb.tile([P, cols], U8, name=name + "_scales", align_bytes=64)
            width = cols // pieces
            for i in range(pieces):
                piece = slice(i * width, (i + 1) * width)
                nc.vector.quantize_mx(
                    out=codes[:, piece].bitcast(FP8X4),
                    scales=scales[:, piece],
                    in_=grouped[:, piece, :].rearrange("p c j -> p (c j)"),
                )
            return codes, scales

        def mx(out, lhs, lhs_cols, rhs, rhs_cols, start, stop):
            nc.tensor.matmul_mx(
                out=out,
                lhsT=lhs[0][:, lhs_cols].bitcast(FP8X4),
                lhsT_scale=lhs[1][:, lhs_cols],
                rhs=rhs[0][:, rhs_cols].bitcast(FP8X4),
                rhs_scale=rhs[1][:, rhs_cols],
                start=start,
                stop=stop,
            )

        def pick(table, offsets, count, dtype, name):
            picked = sb.tile([P, count], dtype, name=name, align_bytes=64)
            nc.vector.tensor_copy(picked[:], table[:].indirect(offsets[:]))
            return picked

        def tiles_view(ap):
            return ap.rearrange("p t (c i) -> p c t i", i=2)

        def interleaved_view(ap):
            return ap.rearrange("p (c i) t -> p c t i", i=2)

        offs_t = load_list(offs, "offs_t")
        w1_left = load_weight(w1, "w1_left", 0, H // 2)
        xs = load_scales(x_scales, "xs")
        xw = load_words(x_words, "xw")
        w1_right = load_weight(w1, "w1_right", H // 2, H)
        usr_t = load_list(usr, "usr_t")
        ew = load_words(e_words, "ew")
        pos, gates = [], []
        for d, src in enumerate((pos1, pos2)):
            pos.append(load_list(src, "pos%d_t" % d))
            gates.append(load_gate(d))
        w2_raw = load_weight(w2, "w2", 0, H)
        pos.append(load_list(pos3, "pos2_t"))
        gates.append(load_gate(2))
        es = load_scales(e_scales, "es")
        w3_raw = load_weight(w3, "w3", 0, N)
        w4_raw = load_weight(w4, "w4", 0, N)

        xq_scales = pick(xs, offs_t, S, U8, "xq_scales")
        xq = (pick(xw, offs_t, S, U32, "xq_codes"), xq_scales)
        w1_shares = [
            (scalar_copy, w1_left[:]),
            (scalar_copy, w1_right[:, :, :W1_SCALAR_COLS]),
            (nc.vector.tensor_copy, w1_right[:, :, W1_SCALAR_COLS:]),
        ]
        w1q = quantize(round_weight("w1", w1_shares), "w1", PACK)
        h = [sb.tile([P, S], F32, name="h%d" % t) for t in range(PACK)]
        passes = [(0, slice(0, S // 2), "bank4"), (0, slice(S // 2, S), "bank0")]
        passes.extend((t, slice(0, S), "bank%d" % t) for t in range(1, PACK))
        for t, cols, tag in passes:
            bank = ps.tile([P, cols.stop - cols.start], F32, name="h_" + tag, tag=tag)
            mx(bank[:], w1q, block(t), xq, cols, True, True)
            nc.scalar.copy(h[t][:, cols], bank[:])
        eq_codes = pick(ew, usr_t, V, U32, "eq_codes")

        def gather(term, t, d):
            nc.vector.tensor_tensor(term[:, t, :], h[t][:].indirect(pos[d][:]), gates[d][:], MULT)

        terms = [sb.tile([P, PACK, V], F32, name="term%d" % d) for d in range(2)]
        for t in range(PACK):
            for d in range(2):
                gather(terms[d], t, d)
        eq = (eq_codes, pick(es, usr_t, V, U8, "eq_scales"))
        part = sb.tile([P, PACK, V], F32, name="part")
        nc.vector.tensor_tensor(part[:], terms[0][:], terms[1][:], ADD)

        w2q = quantize(round_weight("w2", [(scalar_copy, w2_raw[:])]), "w2")
        gg = []
        for half in range(HALVES):
            bank = ps.tile([P, PACK, VH], F32, name="gg%d" % half, tag="gg%d" % half)
            for t in range(PACK):
                mx(bank[:, t, :], w2q, block(t), eq, block(half), True, True)
            gg.append(bank)

        last = sb.tile([P, PACK, V], F32, name="term2", tag="w2_bf", align_bytes=64)
        for t in range(PACK):
            gather(last, t, 2)
        w3q = quantize(round_weight("w3", [(scalar_copy, w3_raw[:])]), "w3")
        w4_bf = round_weight("w4", [(scalar_copy, w4_raw[:])])

        z = sb.tile([P, HALVES, PACK, VH], F32, name="z", tag="w4_raw", align_bytes=64)

        def add_last(half):
            nc.vector.tensor_tensor(z[:, half], part[:, :, block(half)], last[:, :, block(half)], ADD)
            z_bf = sb.tile([P, VH, PACK], BF16, name="z_bf%d" % half, align_bytes=64)
            nc.scalar.copy(interleaved_view(z_bf[:]), tiles_view(z[:, half]))
            return z_bf

        def times_gg(half):
            y_bf = sb.tile([P, VH, PACK], BF16, name="y_bf%d" % half, align_bytes=64)
            nc.vector.tensor_tensor(interleaved_view(y_bf[:]), tiles_view(z[:, half]), tiles_view(gg[half][:]), MULT)
            return y_bf

        z_bf0 = add_last(0)
        w4q = quantize(w4_bf, "w4")
        zq0 = quantize(z_bf0[:], "z0")
        y_bf0 = times_gg(0)
        z_bf1 = add_last(1)
        yq0 = quantize(y_bf0[:], "y0")
        y_bf1 = times_gg(1)
        zq1 = quantize(z_bf1[:], "z1")
        yq1 = quantize(y_bf1[:], "y1")

        out_rows = out_0.rearrange("(p t) v -> p t v", t=PACK)
        out_words = out_1[0].rearrange("p c r -> p (c r)").bitcast(I32)
        out_scales = sb.tile([P, V], U8, name="out_scales", align_bytes=64)

        def finish(half, zq, yq, tags):
            res = sb.tile([P, PACK, VH], F32, name="res%d" % half)
            banks = [ps.tile([P, VH], F32, name="res_bank%d_%d" % (half, t), tag=tags[t]) for t in range(PACK)]
            for t in range(PACK):
                mx(banks[t][:], w3q, block(t), zq, slice(0, VH), True, False)
            for t in range(PACK):
                mx(banks[t][:], w4q, block(t), yq, slice(0, VH), False, True)
                nc.scalar.activation(res[:, t, :], banks[t][:], RELU)
            nc.sync.dma_start(out_rows[:, :, block(half)], res[:])
            return res

        def hand_on(half, res):
            res_bf = sb.tile([P, VH, PACK], BF16, name="res_bf%d" % half, align_bytes=64)
            nc.vector.tensor_copy(interleaved_view(res_bf[:]), tiles_view(res[:]))
            codes = sb.tile([P, VH], U32, name="out_codes%d" % half, align_bytes=64)
            nc.vector.quantize_mx(
                out=codes[:].bitcast(FP8X4),
                scales=out_scales[:, block(half)],
                in_=res_bf[:].rearrange("p v t -> p (v t)"),
            )
            nc.sync.dma_start(out_words[:, block(half)], codes[:].bitcast(I32))

        res0 = finish(0, zq0, yq0, ["bank0", "bank1", "bank2", "bank3"])
        res1 = finish(1, zq1, yq1, ["bank4", "bank5", "gg0", "gg1"])
        hand_on(0, res0)
        hand_on(1, res1)
        for q in range(QUADRANTS):
            queue = nc.scalar if q % 2 else nc.sync
            queue.dma_start(
                out_2[0, 4 * q : 4 * q + 4, :].bitcast(I32), out_scales[32 * q : 32 * q + 4, :].bitcast(I32)
            )
